import numpy as np
import ml_dtypes


def mxq(x, axis, fmt="e4m3"):
    dtype, down = {"e4m3": (ml_dtypes.float8_e4m3fn, 7), "e5m2": (ml_dtypes.float8_e5m2, 14)}[fmt]
    v = np.moveaxis(np.asarray(x, np.float32).astype(ml_dtypes.bfloat16).astype(np.float64), axis, -1)
    blocks = v.reshape(v.shape[:-1] + (-1, 32))
    amax = np.abs(blocks).max(-1, keepdims=True)
    byte = np.maximum(np.where(amax > 0, np.frexp(amax)[1] - 1 + 127, 0) - down, 1)
    scale = np.exp2(byte - 127.0)
    codes = (blocks / scale).astype(np.float32).astype(dtype).astype(np.float64)
    return np.moveaxis((codes * scale).reshape(v.shape), -1, axis)


WIDE = False


def mx_kscale(k):
    if not WIDE:
        return np.ones(k)
    levels = np.array([30, -30])
    if k % 512:
        return np.exp2(np.random.permutation(np.resize(levels, k // 32))).repeat(32)
    a = np.empty((k // 512, 16))
    for p in range(k // 512):
        a[p, :8] = np.random.permutation(np.resize(levels, 8))
        for g in range(8):
            far = levels[np.abs(levels - a[p, g]) >= 10]
            a[p, g + 8] = far[np.random.randint(len(far))]
    return np.exp2(a.ravel()).repeat(32)


def f64(x):
    return np.asarray(x).astype(np.float64)


E2M1 = np.array([0.0, 0.5, 1.0, 1.5, 2.0, 3.0, 4.0, 6.0, -0.0, -0.5, -1.0, -1.5, -2.0, -3.0, -4.0, -6.0])


def pack_weight(w, fmt):
    k, n = w.shape
    w = f64(np.asarray(w, np.float32).astype(ml_dtypes.bfloat16)).reshape(k // 32, 32, n)
    amax = np.abs(w).max(1)
    if fmt == "e4m3":
        byte = np.frexp(amax)[1] - 1 + 127 - 7
    else:
        mant, ex = np.frexp(amax / 6.0)
        byte = np.where(mant > 0.5, ex, ex - 1) + 127
    byte = np.clip(np.where(amax > 0, byte, 1), 1, 254)
    scaled = (w * np.exp2(127.0 - byte)[:, None, :]).reshape(k, n).astype(np.float32)
    by_word = np.ascontiguousarray(scaled.reshape(k // 512, 128, 4, n).transpose(0, 1, 3, 2))
    if fmt == "e4m3":
        words = by_word.astype(ml_dtypes.float8_e4m3fn).view(np.uint8)
    else:
        c = by_word.astype(ml_dtypes.float4_e2m1fn).view(np.uint8) & 0xF
        words = (c[..., 0::2] | (c[..., 1::2] << 4)).reshape(k // 512, 128, 2 * n)
    return np.ascontiguousarray(words), np.ascontiguousarray(byte.astype(np.uint8).reshape(k // 512, 16, n))


def unpack_weight(words, scales, fmt):
    g, _, n = scales.shape
    words = np.ascontiguousarray(words).reshape(g, 128, n, -1)
    if fmt == "e4m3":
        vals = words.view(ml_dtypes.float8_e4m3fn).astype(np.float64)
    else:
        nib = np.empty((g, 128, n, 4), np.uint8)
        nib[..., 0::2] = words & 0xF
        nib[..., 1::2] = words >> 4
        vals = E2M1[nib]
    vals = vals * np.repeat(np.exp2(scales.astype(np.float64) - 127.0), 8, axis=1)[..., None]
    return vals.transpose(0, 1, 3, 2).reshape(g * 512, n)


def planes(y):
    n, m = y.shape
    v = y.astype(np.float32).astype(ml_dtypes.bfloat16).astype(np.float64).reshape(n // 32, 32, m)
    top = np.abs(v).max(1)
    byte = np.clip(np.where(top > 0, np.frexp(top)[1] - 1 + 127 - 7, 1), 1, 254)
    codes = (v * np.exp2(127.0 - byte)[:, None, :]).reshape(n, m).astype(np.float32).astype(ml_dtypes.float8_e4m3fn).view(np.uint8)
    words = codes.reshape(n // 512, 128, 4, m).transpose(0, 1, 3, 2)
    return np.ascontiguousarray(words), np.ascontiguousarray(byte.astype(np.uint8).reshape(n // 512, 16, m))


def gelu(v):
    return 0.5 * v * (1.0 + np.tanh(np.sqrt(2.0 / np.pi) * (v + 0.044715 * v**3)))


K, L, R, M, T = 1536, 512, 1024, 1024, 512


def setup_inputs():
    n = np.random.standard_normal
    s1 = mx_kscale(K)[:, None]
    s2 = mx_kscale(L)[:, None]
    u = mx_kscale(R)[:, None]
    p_w = pack_weight(n((R, M)) / np.sqrt(R) / u, "e2m1")
    return {
        "x": (n((K, T)) * s1).astype(np.float32),
        "wx": (n((K, R)) / np.sqrt(K) / s1 * u.T).astype(np.float32),
        "c": (n((L, T)) * s2).astype(np.float32),
        "wc": (n((L, R)) / np.sqrt(L) / s2).astype(np.float32),
        "w_words": p_w[0],
        "w_scales": p_w[1],
        "b": (0.3 * n(1024)).astype(np.float32),
    }


def reference(x, wx, c, wc, w_words, w_scales, b):
    x_ = mxq(f64(x), 0, "e4m3")
    wx_ = mxq(f64(wx), 0, "e4m3")
    c_ = mxq(f64(c), 0, "e5m2")
    wc_ = mxq(f64(wc), 0, "e4m3")
    w_ = unpack_weight(w_words, w_scales, "e2m1")
    h_ = mxq((wx_.T @ x_) * (wc_.T @ c_), 0, "e4m3")
    y = w_.T @ h_
    out_0 = gelu(y + f64(b)[:, None])
    return (out_0,) + planes(out_0)

@@ -1,0 +1,245 @@
+from contextlib import ExitStack
+
+import concourse.mybir as mybir
+
+K, L, R, M, T = 1536, 512, 1024, 1024, 512
+FLOPS = 2 * T * (K * R + L * R + R * M)
+
+F32 = mybir.dt.float32
+BF16 = mybir.dt.bfloat16
+U32 = mybir.dt.uint32
+I32 = mybir.dt.int32
+U8 = mybir.dt.uint8
+E4M3 = mybir.dt.float8_e4m3fn_x4
+E5M2 = mybir.dt.float8_e5m2_x4
+E2M1 = mybir.dt.float4_e2m1fn_x4
+GELU = mybir.ActivationFunctionType.Gelu_apprx_tanh
+MULT = mybir.AluOpType.mult
+
+P = 128
+PACK = 4
+PASS = 512
+TQ = 128
+TH = 256
+
+SHARE = {'c': 8, 'wc0': 16, 'wc1': 20, 'wx00': 26, 'wx01': 26, 'wx02': 24, 'wx10': 22, 'x00': 16, 'x01': 16, 'x02': 16, 'wx11': 20, 'wx12': 20, 'x10': 0, 'x11': 0, 'x12': 8, 'r00': 32, 'r01': 32, 'r10': 32, 'r11': 32, 'r20': 32, 'r21': 32, 'r30': 32, 'r31': 32}
+LOADS = ['c', 'wc0', 'wc1', 'wx00', 'wx01', 'wx02', 'wx10', 'x00', 'x01', 'x02', 'wx11', 'wx12', 'x10', 'x11', 'x12']
+ORDER = [
+    ('dw', 0, 0), ('dw', 0, 1), ('dw', 1, 0), ('dw', 1, 1), ('cs', 'c'), ('cv', 'c'),
+    ('ds',), ('q', 'c'), ('cs', 'wc0'), ('cv', 'wc0'), ('q', 'wc0'), ('pc', 0),
+    ('cs', 'wc1'), ('cv', 'wc1'), ('q', 'wc1'), ('pc', 1), ('dc', 0, 0), ('dc', 0, 1),
+    ('cs', 'wx00'), ('cv', 'wx00'), ('q', 'wx00'), ('dc', 0, 2), ('dc', 0, 3), ('dc', 1, 0),
+    ('cs', 'wx01'), ('cv', 'wx01'), ('q', 'wx01'), ('dc', 1, 1), ('dc', 1, 2), ('cs', 'wx02'),
+    ('cv', 'wx02'), ('q', 'wx02'), ('dc', 1, 3), ('cs', 'wx10'), ('cv', 'wx10'), ('q', 'wx10'),
+    ('cs', 'x00'), ('cv', 'x00'), ('q', 'x00'), ('cs', 'x01'), ('cv', 'x01'), ('q', 'x01'),
+    ('cs', 'x02'), ('cv', 'x02'), ('q', 'x02'), ('px', 0, 0), ('px', 1, 0), ('cs', 'wx11'),
+    ('cv', 'wx11'), ('q', 'wx11'), ('mu', 0, 0), ('cs', 'wx12'), ('cv', 'wx12'), ('q', 'wx12', 0, 4),
+    ('q', 'wx12', 1, 4), ('q', 'wx12', 2, 4), ('q', 'wx12', 3, 4), ('px', 0, 1), ('px', 1, 1), ('cs', 'x10'),
+    ('cv', 'x10'), ('mu', 1, 0), ('qh', 0, 0), ('mu', 0, 1), ('q', 'x10'), ('qh', 0, 1),
+    ('qh', 1, 0), ('cs', 'x11'), ('cv', 'x11'), ('cs', 'x12'), ('ph', 0, 0), ('ph', 0, 1),
+    ('cv', 'x12'), ('q', 'x11'), ('mu', 1, 1), ('q', 'x12'), ('qh', 1, 1), ('act', 0, 0),
+    ('st', 0, 0), ('act', 0, 1), ('st', 0, 1), ('px', 2, 0), ('px', 2, 1), ('ph', 1, 0),
+    ('ph', 1, 1), ('cr', 0, 0), ('cr', 0, 1), ('mu', 2, 0), ('qr', 0, 0), ('qr', 0, 1),
+    ('sw', 0), ('mu', 2, 1), ('qh', 2, 0), ('qh', 2, 1), ('act', 1, 0), ('st', 1, 0),
+    ('act', 1, 1), ('st', 1, 1), ('px', 3, 0), ('px', 3, 1), ('ph', 2, 0), ('ph', 2, 1),
+    ('cr', 1, 0), ('mu', 3, 0), ('cr', 1, 1), ('mu', 3, 1), ('qh', 3, 0), ('qh', 3, 1),
+    ('qr', 1, 0), ('qr', 1, 1), ('sw', 1), ('ph', 3, 0), ('ph', 3, 1), ('act', 2, 0),
+    ('st', 2, 0), ('act', 2, 1), ('st', 2, 1), ('act', 3, 0), ('st', 3, 0), ('cr', 2, 0),
+    ('cr', 2, 1), ('qr', 2, 0), ('qr', 2, 1), ('sw', 2), ('act', 3, 1), ('st', 3, 1),
+    ('cr', 3, 0), ('cr', 3, 1), ('qr', 3, 0), ('qr', 3, 1), ('sw', 3),
+]
+
+
+def tile_mix_bilin_fm_pl_gelu_kernel(tc, x, wx, c, wc, w_words, w_scales, b, out_0, out_1, out_2):
+    nc = tc.nc
+    with ExitStack() as ctx:
+        keep = ctx.enter_context(tc.tile_pool(name="keep", bufs=1))
+        stage = ctx.enter_context(tc.tile_pool(name="stage", bufs=4))
+        psum = ctx.enter_context(tc.psum_pool(name="psum", bufs=1))
+        ctx.enter_context(tc.manual_schedule())
+
+        banks_taken = []
+
+        def take_bank(name):
+            tag = "bank%d" % (len(banks_taken) % 8)
+            banks_taken.append(name)
+            return psum.tile([P, PASS], F32, name=name, tag=tag)
+
+        raw, grouped, codes, scales = {}, {}, {}, {}
+
+        def load(key, rows):
+            width = rows.shape[1]
+            raw[key] = keep.tile([P, PACK, width], F32, name="raw_" + key)
+            nc.sync.dma_start(out=raw[key][:], in_=rows.rearrange("(p k) n -> p k n", k=PACK))
+
+        def cast_views(key):
+            width = raw[key].shape[2]
+            if key not in grouped:
+                grouped[key] = stage.tile([P, PACK * width], BF16, name="grouped_" + key, tag="grouped%d" % width, align_bytes=64)
+            if key.startswith("w"):
+                dst = grouped[key][:].rearrange("p (j m k) -> p m k j", j=PACK, k=PACK)
+            else:
+                dst = grouped[key][:].rearrange("p (m j k) -> p m k j", j=PACK, k=PACK)
+            src = raw[key][:].rearrange("p k (m j) -> p m k j", j=PACK)
+            groups = width // PACK
+            return dst, src, groups * SHARE[key] // 32, groups
+
+        def cast_s(key):
+            dst, src, cut, groups = cast_views(key)
+            if cut < groups:
+                nc.scalar.copy(out=dst[:, cut:groups], in_=src[:, cut:groups])
+
+        def cast_v(key):
+            dst, src, cut, groups = cast_views(key)
+            if cut > 0:
+                nc.vector.tensor_copy(out=dst[:, 0:cut], in_=src[:, 0:cut])
+
+        def quantize(key, part=0, parts=1):
+            width = raw[key].shape[2]
+            fmt = E5M2 if key == "c" else E4M3
+            if key not in codes:
+                codes[key] = keep.tile([P, width], U32, name="codes_" + key, align_bytes=64)
+                scales[key] = keep.tile([P, width], U8, name="scales_" + key, align_bytes=64)
+            lo, hi = part * width // parts, (part + 1) * width // parts
+            nc.vector.quantize_mx(out=codes[key][:, lo:hi].bitcast(fmt), scales=scales[key][:, lo:hi], in_=grouped[key][:, PACK * lo : PACK * hi])
+
+        ws_raw = keep.tile([P, 2, M], U8, name="ws_raw")
+        nc.vector.memset(ws_raw[:].rearrange("p a n -> p (a n)").bitcast(I32), 0)
+        warm = keep.tile([P, 8], F32, name="warm")
+        warm_out = keep.tile([P, 8], F32, name="warm_out")
+        nc.vector.memset(warm[:], 0.0)
+        bias = keep.tile([P, 2, PACK], F32, name="bias")
+        nc.scalar.dma_start(out=bias[:], in_=b.rearrange("(h p i) -> p h i", h=2, i=PACK))
+        for quad in range(4):
+            nc.scalar.dma_start(
+                out=ws_raw[32 * quad : 32 * quad + 4, :, :].bitcast(I32),
+                in_=w_scales[:, 4 * quad : 4 * quad + 4, :].rearrange("a r n -> r a n").bitcast(I32),
+            )
+        nc.scalar.activation(out=warm_out[:, 0:1], in_=warm[:, 0:1], func=GELU)
+        ww_raw = keep.tile([P, 2, 2 * M], U8, name="ww_raw")
+        nc.sync.dma_start(out=ww_raw[:].bitcast(I32), in_=w_words.rearrange("a p n -> p a n").bitcast(I32))
+
+        def load_wx(a, g):
+            load("wx%d%d" % (a, g), wx[g * PASS : (g + 1) * PASS, a * PASS : (a + 1) * PASS])
+
+        def load_x(half, g):
+            load("x%d%d" % (half, g), x[g * PASS : (g + 1) * PASS, half * TH : (half + 1) * TH])
+
+        for key in LOADS:
+            if key == "c":
+                load("c", c)
+            elif key.startswith("wc"):
+                load(key, wc[:, int(key[2]) * PASS : (int(key[2]) + 1) * PASS])
+            elif key.startswith("wx"):
+                load_wx(int(key[2]), int(key[3]))
+            else:
+                load_x(int(key[1]), int(key[2]))
+
+        ww = keep.tile([P, 2, 2 * M], U8, name="ww", align_bytes=64)
+        ws = keep.tile([P, 2, M], U8, name="ws", align_bytes=64)
+
+        def deal_words(a, h):
+            cols = slice(2 * PASS * h, 2 * PASS * (h + 1))
+            nc.vector.tensor_copy(
+                out=ww[:, a, cols].rearrange("p (i m e) -> p i m e", i=PACK, e=2),
+                in_=ww_raw[:, a, cols].rearrange("p (m i e) -> p i m e", i=PACK, e=2),
+            )
+
+        def deal_scales():
+            nc.vector.tensor_copy(
+                out=ws[:].rearrange("p a (h i m) -> p (a h) i m", h=2, i=PACK),
+                in_=ws_raw[:].rearrange("p a (h m i) -> p (a h) i m", h=2, i=PACK),
+            )
+
+        pc = {}
+
+        def project_c(a):
+            pc[a] = keep.tile([P, PACK, T], F32, name="pc%d" % a)
+            for j in range(PACK):
+                acc = take_bank("pc_acc%d%d" % (a, j))
+                cols = slice(j * P, (j + 1) * P)
+                key = "wc%d" % a
+                nc.tensor.matmul_mx(out=acc[:], lhsT=codes[key][:, cols].bitcast(E4M3), lhsT_scale=scales[key][:, cols],
+                                    rhs=codes["c"][:].bitcast(E5M2), rhs_scale=scales["c"][:], start=True, stop=True)
+                pc_acc[a, j] = acc
+
+        pc_acc = {}
+
+        def drain_c(a, j):
+            nc.scalar.copy(out=pc[a][:, j, :], in_=pc_acc[a, j][:])
+
+        px_acc, h_bf, h_codes, h_scales = {}, {}, {}, {}
+
+        def project_x(q, a):
+            acc = take_bank("px_acc%d%d" % (q, a))
+            px_acc[q, a] = acc
+            tcols = slice((q % 2) * TQ, (q % 2 + 1) * TQ)
+            for j in range(PACK):
+                cols = slice(j * P, (j + 1) * P)
+                for g in range(3):
+                    wkey, xkey = "wx%d%d" % (a, g), "x%d%d" % (q // 2, g)
+                    nc.tensor.matmul_mx(out=acc[:, cols], lhsT=codes[wkey][:, cols].bitcast(E4M3), lhsT_scale=scales[wkey][:, cols],
+                                        rhs=codes[xkey][:, tcols].bitcast(E4M3), rhs_scale=scales[xkey][:, tcols],
+                                        start=(g == 0), stop=(g == 2))
+
+        def multiply(q, a):
+            h_bf[q, a] = stage.tile([P, PACK * TQ], BF16, name="h_bf%d%d" % (q, a), tag="h_bf", align_bytes=64)
+            nc.vector.tensor_tensor(
+                out=h_bf[q, a][:].rearrange("p (m i j) -> p m j i", i=PACK, j=PACK),
+                in0=px_acc[q, a][:].rearrange("p (j m i) -> p m j i", j=PACK, i=PACK),
+                in1=pc[a][:, :, q * TQ : (q + 1) * TQ].rearrange("p j (m i) -> p m j i", i=PACK),
+                op=MULT,
+            )
+
+        def quantize_h(q, a):
+            h_codes[q, a] = keep.tile([P, TQ], U32, name="h_codes%d%d" % (q, a), align_bytes=64)
+            h_scales[q, a] = keep.tile([P, TQ], U8, name="h_scales%d%d" % (q, a), align_bytes=64)
+            nc.vector.quantize_mx(out=h_codes[q, a][:].bitcast(E4M3), scales=h_scales[q, a][:], in_=h_bf[q, a][:])
+
+        y_acc, res, res_bf, res_codes = {}, {}, {}, {}
+        res_scales = keep.tile([P, 2, T], U8, name="res_scales", align_bytes=64)
+
+        def project_h(q, h):
+            acc = take_bank("y_acc%d%d" % (q, h))
+            y_acc[q, h] = acc
+            for i in range(PACK):
+                n0 = h * PASS + i * P
+                for a in range(2):
+                    nc.tensor.matmul_mx(out=acc[:, i * TQ : (i + 1) * TQ], lhsT=ww[:, a, 2 * n0 : 2 * (n0 + P)].bitcast(E2M1),
+                                        lhsT_scale=ws[:, a, n0 : n0 + P], rhs=h_codes[q, a][:].bitcast(E4M3),
+                                        rhs_scale=h_scales[q, a][:], start=(a == 0), stop=(a == 1))
+
+        def activate(q, h):
+            res[q, h] = keep.tile([P, PACK, TQ], F32, name="res%d%d" % (q, h))
+            for i in range(PACK):
+                nc.scalar.activation(out=res[q, h][:, i, :], in_=y_acc[q, h][:, i * TQ : (i + 1) * TQ], func=GELU, bias=bias[:, h, i : i + 1])
+
+        def store_res(q, h):
+            rows = out_0[h * PASS : (h + 1) * PASS, q * TQ : (q + 1) * TQ]
+            nc.sync.dma_start(out=rows.rearrange("(p i) t -> p i t", i=PACK), in_=res[q, h][:])
+
+        def cast_res(q, h):
+            res_bf[q, h] = stage.tile([P, PACK * TQ], BF16, name="res_bf%d%d" % (q, h), tag="res_bf", align_bytes=64)
+            nc.vector.tensor_copy(
+                out=res_bf[q, h][:].rearrange("p (m j i) -> p m i j", j=PACK, i=PACK),
+                in_=res[q, h][:].rearrange("p i (m j) -> p m i j", j=PACK),
+            )
+
+        def quantize_res(q, h):
+            if q not in res_codes:
+                res_codes[q] = keep.tile([P, 2, TQ], U32, name="res_codes%d" % q, align_bytes=64)
+            nc.vector.quantize_mx(out=res_codes[q][:, h, :].bitcast(E4M3), scales=res_scales[:, h, q * TQ : (q + 1) * TQ], in_=res_bf[q, h][:])
+
+        def store_words(q):
+            words = out_1.rearrange("h p t i -> p h (t i)").bitcast(I32)
+            nc.sync.dma_start(out=words[:, :, q * TQ : (q + 1) * TQ], in_=res_codes[q][:].bitcast(I32))
+
+        steps = {"cs": cast_s, "cv": cast_v, "q": quantize, "dw": deal_words, "ds": deal_scales, "pc": project_c, "dc": drain_c, "px": project_x,
+                 "mu": multiply, "qh": quantize_h, "ph": project_h, "act": activate, "st": store_res, "cr": cast_res, "qr": quantize_res, "sw": store_words}
+        for step in ORDER:
+            steps[step[0]](*step[1:])
+        for quad in range(4):
+            nc.sync.dma_start(
+                out=out_2[:, 4 * quad : 4 * quad + 4, :].rearrange("h r t -> r h t").bitcast(I32),
+                in_=res_scales[32 * quad : 32 * quad + 4, :, :].bitcast(I32),
+            )

@@ -22,31 +22,31 @@ PASS = 512
 TQ = 128
 TH = 256
 
-SHARE = {'c': 8, 'wc0': 16, 'wc1': 20, 'wx00': 26, 'wx01': 26, 'wx02': 24, 'wx10': 22, 'x00': 16, 'x01': 16, 'x02': 16, 'wx11': 20, 'wx12': 20, 'x10': 0, 'x11': 0, 'x12': 8, 'r00': 32, 'r01': 32, 'r10': 32, 'r11': 32, 'r20': 32, 'r21': 32, 'r30': 32, 'r31': 32}
-LOADS = ['c', 'wc0', 'wc1', 'wx00', 'wx01', 'wx02', 'wx10', 'x00', 'x01', 'x02', 'wx11', 'wx12', 'x10', 'x11', 'x12']
+SHARE = {'c': 8, 'wc0': 20, 'wc1': 20, 'wx00': 20, 'wx10': 20, 'wx01': 20, 'wx11': 20, 'wx02': 20, 'x00': 16, 'x01': 16, 'x02': 20, 'wx12': 20, 'x10': 0, 'x11': 0, 'x12': 20, 'r00': 32, 'r01': 32, 'r10': 32, 'r11': 32, 'r20': 32, 'r21': 32, 'r30': 32, 'r31': 32}
+LOADS = ['c', 'wc', 'wxg0', 'wxg1', 'wx02', 'x00', 'x01', 'x02', 'wx12', 'x10', 'x11', 'x12']
 ORDER = [
     ('dw', 0, 0), ('dw', 0, 1), ('dw', 1, 0), ('dw', 1, 1), ('cs', 'c'), ('cv', 'c'),
-    ('ds',), ('q', 'c'), ('cs', 'wc0'), ('cv', 'wc0'), ('q', 'wc0'), ('pc', 0),
-    ('cs', 'wc1'), ('cv', 'wc1'), ('q', 'wc1'), ('pc', 1), ('dc', 0, 0), ('dc', 0, 1),
-    ('cs', 'wx00'), ('cv', 'wx00'), ('q', 'wx00'), ('dc', 0, 2), ('dc', 0, 3), ('dc', 1, 0),
-    ('cs', 'wx01'), ('cv', 'wx01'), ('q', 'wx01'), ('dc', 1, 1), ('dc', 1, 2), ('cs', 'wx02'),
-    ('cv', 'wx02'), ('q', 'wx02'), ('dc', 1, 3), ('cs', 'wx10'), ('cv', 'wx10'), ('q', 'wx10'),
-    ('cs', 'x00'), ('cv', 'x00'), ('q', 'x00'), ('cs', 'x01'), ('cv', 'x01'), ('q', 'x01'),
-    ('cs', 'x02'), ('cv', 'x02'), ('q', 'x02'), ('px', 0, 0), ('px', 1, 0), ('cs', 'wx11'),
-    ('cv', 'wx11'), ('q', 'wx11'), ('mu', 0, 0), ('cs', 'wx12'), ('cv', 'wx12'), ('q', 'wx12', 0, 4),
+    ('ds',), ('q', 'c'), ('cs', 'wc0'), ('cv', 'wc0'), ('cs', 'wc1'), ('cv', 'wc1'),
+    ('q', 'wc0'), ('q', 'wc1'), ('pc', 0), ('dc', 0, 0), ('dc', 0, 1), ('dc', 0, 2),
+    ('cs', 'wx00'), ('cv', 'wx00'), ('cs', 'wx10'), ('cv', 'wx10'), ('q', 'wx00'), ('q', 'wx10'),
+    ('dc', 0, 3), ('cs', 'wx01'), ('cv', 'wx01'), ('cs', 'wx11'), ('cv', 'wx11'), ('q', 'wx01'),
+    ('q', 'wx11'), ('cs', 'wx02'), ('cv', 'wx02'), ('q', 'wx02'), ('cs', 'x00'), ('cv', 'x00'),
+    ('q', 'x00'), ('px', 0, 0, 0, 1), ('cs', 'x01'), ('cv', 'x01'), ('q', 'x01'), ('pc', 1),
+    ('cs', 'x02'), ('cv', 'x02'), ('q', 'x02'), ('px', 0, 0, 1, 12), ('px', 1, 0), ('dc', 1, 0),
+    ('dc', 1, 1), ('dc', 1, 2), ('cs', 'wx12'), ('dc', 1, 3), ('cv', 'wx12'), ('q', 'wx12', 0, 4),
     ('q', 'wx12', 1, 4), ('q', 'wx12', 2, 4), ('q', 'wx12', 3, 4), ('px', 0, 1), ('px', 1, 1), ('cs', 'x10'),
-    ('cv', 'x10'), ('mu', 1, 0), ('qh', 0, 0), ('mu', 0, 1), ('q', 'x10'), ('qh', 0, 1),
-    ('qh', 1, 0), ('cs', 'x11'), ('cv', 'x11'), ('cs', 'x12'), ('ph', 0, 0), ('ph', 0, 1),
-    ('cv', 'x12'), ('q', 'x11'), ('mu', 1, 1), ('q', 'x12'), ('qh', 1, 1), ('act', 0, 0),
-    ('st', 0, 0), ('act', 0, 1), ('st', 0, 1), ('px', 2, 0), ('px', 2, 1), ('ph', 1, 0),
-    ('ph', 1, 1), ('cr', 0, 0), ('cr', 0, 1), ('mu', 2, 0), ('qr', 0, 0), ('qr', 0, 1),
-    ('sw', 0), ('mu', 2, 1), ('qh', 2, 0), ('qh', 2, 1), ('act', 1, 0), ('st', 1, 0),
-    ('act', 1, 1), ('st', 1, 1), ('px', 3, 0), ('px', 3, 1), ('ph', 2, 0), ('ph', 2, 1),
-    ('cr', 1, 0), ('mu', 3, 0), ('cr', 1, 1), ('mu', 3, 1), ('qh', 3, 0), ('qh', 3, 1),
-    ('qr', 1, 0), ('qr', 1, 1), ('sw', 1), ('ph', 3, 0), ('ph', 3, 1), ('act', 2, 0),
-    ('st', 2, 0), ('act', 2, 1), ('st', 2, 1), ('act', 3, 0), ('st', 3, 0), ('cr', 2, 0),
-    ('cr', 2, 1), ('qr', 2, 0), ('qr', 2, 1), ('sw', 2), ('act', 3, 1), ('st', 3, 1),
-    ('cr', 3, 0), ('cr', 3, 1), ('qr', 3, 0), ('qr', 3, 1), ('sw', 3),
+    ('cv', 'x10'), ('mu', 0, 0), ('mu', 0, 1), ('qh', 0, 0), ('qh', 0, 1), ('mu', 1, 0),
+    ('mu', 1, 1), ('qh', 1, 0), ('qh', 1, 1), ('cs', 'x11'), ('cv', 'x11'), ('q', 'x10'),
+    ('cs', 'x12'), ('cv', 'x12'), ('q', 'x11'), ('q', 'x12'), ('ph', 0, 0), ('ph', 0, 1),
+    ('ph', 1, 0), ('ph', 1, 1), ('act', 0, 0), ('st', 0, 0), ('act', 0, 1), ('st', 0, 1),
+    ('act', 1, 0), ('st', 1, 0), ('act', 1, 1), ('st', 1, 1), ('px', 2, 0), ('px', 2, 1),
+    ('px', 3, 0), ('px', 3, 1), ('cr', 0, 0), ('cr', 0, 1), ('qr', 0, 0), ('cr', 1, 0),
+    ('qr', 0, 1), ('sw', 0), ('mu', 2, 0), ('cr', 1, 1), ('mu', 2, 1), ('qh', 2, 0),
+    ('qr', 1, 0), ('qh', 2, 1), ('mu', 3, 0), ('qr', 1, 1), ('sw', 1), ('mu', 3, 1),
+    ('qh', 3, 0), ('qh', 3, 1), ('ph', 2, 0), ('ph', 2, 1), ('ph', 3, 0), ('ph', 3, 1),
+    ('act', 2, 0), ('st', 2, 0), ('act', 2, 1), ('st', 2, 1), ('act', 3, 0), ('st', 3, 0),
+    ('cr', 2, 0), ('cr', 2, 1), ('qr', 2, 0), ('qr', 2, 1), ('sw', 2), ('act', 3, 1),
+    ('st', 3, 1), ('cr', 3, 0), ('cr', 3, 1), ('qr', 3, 0), ('qr', 3, 1), ('sw', 3),
 ]
 
 
@@ -80,7 +80,7 @@ def tile_mix_bilin_fm_pl_gelu_kernel(tc, x, wx, c, wc, w_words, w_scales, b, out
                 dst = grouped[key][:].rearrange("p (j m k) -> p m k j", j=PACK, k=PACK)
             else:
                 dst = grouped[key][:].rearrange("p (m j k) -> p m k j", j=PACK, k=PACK)
-            src = raw[key][:].rearrange("p k (m j) -> p m k j", j=PACK)
+            src = raw[key][:, :, :].rearrange("p k (m j) -> p m k j", j=PACK)
             groups = width // PACK
             return dst, src, groups * SHARE[key] // 32, groups
 
@@ -128,6 +128,13 @@ def tile_mix_bilin_fm_pl_gelu_kernel(tc, x, wx, c, wc, w_words, w_scales, b, out
         for key in LOADS:
             if key == "c":
                 load("c", c)
+            elif key == "wc":
+                load(key, wc)
+                raw["wc0"], raw["wc1"] = raw[key][:, :, 0:PASS], raw[key][:, :, PASS : 2 * PASS]
+            elif key.startswith("wxg"):
+                g = int(key[3])
+                load(key, wx[g * PASS : (g + 1) * PASS, :])
+                raw["wx0%d" % g], raw["wx1%d" % g] = raw[key][:, :, 0:PASS], raw[key][:, :, PASS : 2 * PASS]
             elif key.startswith("wc"):
                 load(key, wc[:, int(key[2]) * PASS : (int(key[2]) + 1) * PASS])
             elif key.startswith("wx"):
@@ -170,17 +177,18 @@ def tile_mix_bilin_fm_pl_gelu_kernel(tc, x, wx, c, wc, w_words, w_scales, b, out
 
         px_acc, h_bf, h_codes, h_scales = {}, {}, {}, {}
 
-        def project_x(q, a):
-            acc = take_bank("px_acc%d%d" % (q, a))
-            px_acc[q, a] = acc
+        def project_x(q, a, first=0, last=12):
+            if first == 0:
+                px_acc[q, a] = take_bank("px_acc%d%d" % (q, a))
+            acc = px_acc[q, a]
             tcols = slice((q % 2) * TQ, (q % 2 + 1) * TQ)
-            for j in range(PACK):
+            for n in range(first, last):
+                j, g = divmod(n, 3)
                 cols = slice(j * P, (j + 1) * P)
-                for g in range(3):
-                    wkey, xkey = "wx%d%d" % (a, g), "x%d%d" % (q // 2, g)
-                    nc.tensor.matmul_mx(out=acc[:, cols], lhsT=codes[wkey][:, cols].bitcast(E4M3), lhsT_scale=scales[wkey][:, cols],
-                                        rhs=codes[xkey][:, tcols].bitcast(E4M3), rhs_scale=scales[xkey][:, tcols],
-                                        start=(g == 0), stop=(g == 2))
+                wkey, xkey = "wx%d%d" % (a, g), "x%d%d" % (q // 2, g)
+                nc.tensor.matmul_mx(out=acc[:, cols], lhsT=codes[wkey][:, cols].bitcast(E4M3), lhsT_scale=scales[wkey][:, cols],
+                                    rhs=codes[xkey][:, tcols].bitcast(E4M3), rhs_scale=scales[xkey][:, tcols],
+                                    start=(g == 0), stop=(g == 2))
 
         def multiply(q, a):
             h_bf[q, a] = stage.tile([P, PACK * TQ], BF16, name="h_bf%d%d" % (q, a), tag="h_bf", align_bytes=64)

@@ -22,31 +22,35 @@ PASS = 512
 TQ = 128
 TH = 256
 
-SHARE = {'c': 8, 'wc0': 20, 'wc1': 20, 'wx00': 20, 'wx10': 20, 'wx01': 20, 'wx11': 20, 'wx02': 20, 'x00': 16, 'x01': 16, 'x02': 20, 'wx12': 20, 'x10': 0, 'x11': 0, 'x12': 20, 'r00': 32, 'r01': 32, 'r10': 32, 'r11': 32, 'r20': 32, 'r21': 32, 'r30': 32, 'r31': 32}
-LOADS = ['c', 'wc', 'wxg0', 'wxg1', 'wx02', 'x00', 'x01', 'x02', 'wx12', 'x10', 'x11', 'x12']
+SHARE = {'c': 16, 'wc0': 20, 'wc1': 20, 'wx00': 20, 'wx10': 20, 'wx01': 20, 'wx11': 20, 'wx02': 20, 'x00': 16, 'x01': 16, 'x02': 20, 'wx12': 20, 'x10': 0, 'x11': 0, 'x12': 20, 'r00': 32, 'r01': 32, 'r10': 32, 'r11': 32, 'r20': 32, 'r21': 32, 'r30': 32, 'r31': 32, 'y20': 0, 'y21': 0, 'y22': 0, 'y30': 0, 'y31': 0, 'y32': 0}
+LOADS = ['c', 'wc', 'wxg0', 'wxg1', 'wx02', 'x00', 'x01', 'x02', 'wx12', 'y20', 'y21', 'y22', 'y30', 'y31', 'y32']
 ORDER = [
     ('dw', 0, 0), ('dw', 0, 1), ('dw', 1, 0), ('dw', 1, 1), ('cs', 'c'), ('cv', 'c'),
-    ('ds',), ('q', 'c'), ('cs', 'wc0'), ('cv', 'wc0'), ('cs', 'wc1'), ('cv', 'wc1'),
-    ('q', 'wc0'), ('q', 'wc1'), ('pc', 0), ('dc', 0, 0), ('dc', 0, 1), ('dc', 0, 2),
-    ('cs', 'wx00'), ('cv', 'wx00'), ('cs', 'wx10'), ('cv', 'wx10'), ('q', 'wx00'), ('q', 'wx10'),
+    ('q', 'c'), ('cs', 'wc0'), ('cv', 'wc0'), ('cs', 'wc1'), ('cv', 'wc1'), ('q', 'wc0'),
+    ('q', 'wc1'), ('pc', 0), ('dc', 0, 0), ('dc', 0, 1), ('dc', 0, 2), ('cs', 'wx00'),
+    ('cv', 'wx00'), ('cs', 'wx10'), ('cv', 'wx10'), ('q', 'wx00'), ('q', 'wx10'), ('ds',),
     ('dc', 0, 3), ('cs', 'wx01'), ('cv', 'wx01'), ('cs', 'wx11'), ('cv', 'wx11'), ('q', 'wx01'),
     ('q', 'wx11'), ('cs', 'wx02'), ('cv', 'wx02'), ('q', 'wx02'), ('cs', 'x00'), ('cv', 'x00'),
     ('q', 'x00'), ('px', 0, 0, 0, 1), ('cs', 'x01'), ('cv', 'x01'), ('q', 'x01'), ('pc', 1),
     ('cs', 'x02'), ('cv', 'x02'), ('q', 'x02'), ('px', 0, 0, 1, 12), ('px', 1, 0), ('dc', 1, 0),
-    ('dc', 1, 1), ('dc', 1, 2), ('cs', 'wx12'), ('dc', 1, 3), ('cv', 'wx12'), ('q', 'wx12', 0, 4),
-    ('q', 'wx12', 1, 4), ('q', 'wx12', 2, 4), ('q', 'wx12', 3, 4), ('px', 0, 1), ('px', 1, 1), ('cs', 'x10'),
-    ('cv', 'x10'), ('mu', 0, 0), ('mu', 0, 1), ('qh', 0, 0), ('qh', 0, 1), ('mu', 1, 0),
-    ('mu', 1, 1), ('qh', 1, 0), ('qh', 1, 1), ('cs', 'x11'), ('cv', 'x11'), ('q', 'x10'),
-    ('cs', 'x12'), ('cv', 'x12'), ('q', 'x11'), ('q', 'x12'), ('ph', 0, 0), ('ph', 0, 1),
-    ('ph', 1, 0), ('ph', 1, 1), ('act', 0, 0), ('st', 0, 0), ('act', 0, 1), ('st', 0, 1),
-    ('act', 1, 0), ('st', 1, 0), ('act', 1, 1), ('st', 1, 1), ('px', 2, 0), ('px', 2, 1),
-    ('px', 3, 0), ('px', 3, 1), ('cr', 0, 0), ('cr', 0, 1), ('qr', 0, 0), ('cr', 1, 0),
-    ('qr', 0, 1), ('sw', 0), ('mu', 2, 0), ('cr', 1, 1), ('mu', 2, 1), ('qh', 2, 0),
-    ('qr', 1, 0), ('qh', 2, 1), ('mu', 3, 0), ('qr', 1, 1), ('sw', 1), ('mu', 3, 1),
-    ('qh', 3, 0), ('qh', 3, 1), ('ph', 2, 0), ('ph', 2, 1), ('ph', 3, 0), ('ph', 3, 1),
-    ('act', 2, 0), ('st', 2, 0), ('act', 2, 1), ('st', 2, 1), ('act', 3, 0), ('st', 3, 0),
-    ('cr', 2, 0), ('cr', 2, 1), ('qr', 2, 0), ('qr', 2, 1), ('sw', 2), ('act', 3, 1),
-    ('st', 3, 1), ('cr', 3, 0), ('cr', 3, 1), ('qr', 3, 0), ('qr', 3, 1), ('sw', 3),
+    ('dc', 1, 1), ('dc', 1, 2), ('cp', 'wx12', 0, 0), ('cp', 'wx12', 0, 1), ('cp', 'wx12', 1, 0), ('cp', 'wx12', 1, 1),
+    ('dc', 1, 3), ('q', 'wx12', 0, 4), ('q', 'wx12', 1, 4), ('q', 'wx12', 2, 4), ('q', 'wx12', 3, 4), ('px', 0, 1),
+    ('px', 1, 1), ('cs', 'y20'), ('mu', 0, 0), ('mu', 0, 1), ('qh', 0, 0), ('cs', 'y21'),
+    ('qh', 0, 1), ('ph', 0, 0), ('ph', 0, 1), ('mu', 1, 0), ('cs', 'y22'), ('q', 'y20'),
+    ('q', 'y21'), ('q', 'y22'), ('px', 2, 0), ('px', 2, 1), ('mu', 1, 1), ('qh', 1, 0),
+    ('cs', 'y30'), ('qh', 1, 1), ('act', 0, 0), ('st', 0, 0), ('cs', 'y31'), ('act', 0, 1),
+    ('st', 0, 1), ('cs', 'y32'), ('cr', 0, 0), ('q', 'y30'), ('q', 'y31'), ('qr', 0, 0),
+    ('mu', 2, 0), ('cr', 0, 1), ('mu', 2, 1), ('qr', 0, 1), ('q', 'y32'), ('ph', 1, 0),
+    ('ph', 1, 1), ('px', 3, 0), ('qh', 2, 0), ('qh', 2, 1), ('act', 1, 0), ('st', 1, 0),
+    ('act', 1, 1), ('st', 1, 1), ('ph', 2, 0), ('px', 3, 1), ('ph', 2, 1), ('cr', 1, 0),
+    ('cr', 1, 1), ('mu', 3, 0), ('qr', 1, 0), ('qr', 1, 1), ('sw', 0, 0), ('sw', 0, 1),
+    ('qh', 3, 0), ('act', 2, 0), ('st', 2, 0), ('mu', 3, 1), ('cr', 2, 0), ('qh', 3, 1),
+    ('p1', 3, 0, 0, 0), ('p1', 3, 0, 1, 0), ('p1', 3, 0, 2, 0), ('p1', 3, 0, 3, 0), ('p1', 3, 1, 0, 0), ('p1', 3, 1, 1, 0),
+    ('p1', 3, 0, 0, 1), ('p1', 3, 0, 1, 1), ('p1', 3, 0, 2, 1), ('p1', 3, 0, 3, 1), ('p1', 3, 1, 0, 1), ('p1', 3, 1, 1, 1),
+    ('act', 2, 1), ('st', 2, 1), ('p1', 3, 1, 2, 0), ('p1', 3, 1, 2, 1), ('p1', 3, 1, 3, 0), ('p1', 3, 1, 3, 1),
+    ('qr', 2, 0), ('cr', 2, 1), ('qr', 2, 1), ('act', 3, 0), ('st', 3, 0), ('act', 3, 1),
+    ('st', 3, 1), ('cr', 3, 0), ('qr', 3, 0), ('sw', 1, 0), ('cr', 3, 1), ('qr', 3, 1),
+    ('sw', 1, 1),
 ]
 
 
@@ -94,6 +98,17 @@ def tile_mix_bilin_fm_pl_gelu_kernel(tc, x, wx, c, wc, w_words, w_scales, b, out
             if cut > 0:
                 nc.vector.tensor_copy(out=dst[:, 0:cut], in_=src[:, 0:cut])
 
+        def cast_pair(key, pair, on_vector):
+            if key not in grouped:
+                grouped[key] = stage.tile([P, PACK * PASS], BF16, name="grouped_" + key, tag="grouped%d" % PASS, align_bytes=64)
+            dst = grouped[key][:].rearrange("p (u l m k) -> p u m k l", u=2, l=2, k=PACK)[:, pair]
+            src = raw[key][:, :, :].rearrange("p k (m u l) -> p u m k l", u=2, l=2)[:, pair]
+            cut = P * SHARE[key] // 32
+            if on_vector:
+                nc.vector.tensor_copy(out=dst[:, 0:cut], in_=src[:, 0:cut])
+            else:
+                nc.scalar.copy(out=dst[:, cut:P], in_=src[:, cut:P])
+
         def quantize(key, part=0, parts=1):
             width = raw[key].shape[2]
             fmt = E5M2 if key == "c" else E4M3
@@ -111,7 +126,7 @@ def tile_mix_bilin_fm_pl_gelu_kernel(tc, x, wx, c, wc, w_words, w_scales, b, out
         bias = keep.tile([P, 2, PACK], F32, name="bias")
         nc.scalar.dma_start(out=bias[:], in_=b.rearrange("(h p i) -> p h i", h=2, i=PACK))
         for quad in range(4):
-            nc.scalar.dma_start(
+            nc.gpsimd.dma_start(
                 out=ws_raw[32 * quad : 32 * quad + 4, :, :].bitcast(I32),
                 in_=w_scales[:, 4 * quad : 4 * quad + 4, :].rearrange("a r n -> r a n").bitcast(I32),
             )
@@ -139,6 +154,9 @@ def tile_mix_bilin_fm_pl_gelu_kernel(tc, x, wx, c, wc, w_words, w_scales, b, out
                 load(key, wc[:, int(key[2]) * PASS : (int(key[2]) + 1) * PASS])
             elif key.startswith("wx"):
                 load_wx(int(key[2]), int(key[3]))
+            elif key.startswith("y"):
+                q, g = int(key[1]), int(key[2])
+                load(key, x[g * PASS : (g + 1) * PASS, q * TQ : (q + 1) * TQ])
             else:
                 load_x(int(key[1]), int(key[2]))
 
@@ -181,11 +199,12 @@ def tile_mix_bilin_fm_pl_gelu_kernel(tc, x, wx, c, wc, w_words, w_scales, b, out
             if first == 0:
                 px_acc[q, a] = take_bank("px_acc%d%d" % (q, a))
             acc = px_acc[q, a]
-            tcols = slice((q % 2) * TQ, (q % 2 + 1) * TQ)
+            alone = "y%d0" % q in LOADS
+            tcols = slice(0, TQ) if alone else slice((q % 2) * TQ, (q % 2 + 1) * TQ)
             for n in range(first, last):
                 j, g = divmod(n, 3)
                 cols = slice(j * P, (j + 1) * P)
-                wkey, xkey = "wx%d%d" % (a, g), "x%d%d" % (q // 2, g)
+                wkey, xkey = "wx%d%d" % (a, g), ("y%d%d" % (q, g) if alone else "x%d%d" % (q // 2, g))
                 nc.tensor.matmul_mx(out=acc[:, cols], lhsT=codes[wkey][:, cols].bitcast(E4M3), lhsT_scale=scales[wkey][:, cols],
                                     rhs=codes[xkey][:, tcols].bitcast(E4M3), rhs_scale=scales[xkey][:, tcols],
                                     start=(g == 0), stop=(g == 2))
@@ -207,43 +226,55 @@ def tile_mix_bilin_fm_pl_gelu_kernel(tc, x, wx, c, wc, w_words, w_scales, b, out
         y_acc, res, res_bf, res_codes = {}, {}, {}, {}
         res_scales = keep.tile([P, 2, T], U8, name="res_scales", align_bytes=64)
 
+        def out_pass(q, h, i, a):
+            n0 = h * PASS + i * P
+            nc.tensor.matmul_mx(out=y_acc[q, h, i], lhsT=ww[:, a, 2 * n0 : 2 * (n0 + P)].bitcast(E2M1),
+                                lhsT_scale=ws[:, a, n0 : n0 + P], rhs=h_codes[q, a][:].bitcast(E4M3),
+                                rhs_scale=h_scales[q, a][:], start=(a == 0), stop=(a == 1))
+
         def project_h(q, h):
             acc = take_bank("y_acc%d%d" % (q, h))
-            y_acc[q, h] = acc
             for i in range(PACK):
-                n0 = h * PASS + i * P
+                y_acc[q, h, i] = acc[:, i * TQ : (i + 1) * TQ]
                 for a in range(2):
-                    nc.tensor.matmul_mx(out=acc[:, i * TQ : (i + 1) * TQ], lhsT=ww[:, a, 2 * n0 : 2 * (n0 + P)].bitcast(E2M1),
-                                        lhsT_scale=ws[:, a, n0 : n0 + P], rhs=h_codes[q, a][:].bitcast(E4M3),
-                                        rhs_scale=h_scales[q, a][:], start=(a == 0), stop=(a == 1))
+                    out_pass(q, h, i, a)
+
+        def project_h_alone(q, h, i, a):
+            if a == 0:
+                acc = take_bank("y_acc%d%d%d" % (q, h, i))
+                y_acc[q, h, i] = acc[:, 0:TQ]
+            out_pass(q, h, i, a)
 
         def activate(q, h):
             res[q, h] = keep.tile([P, PACK, TQ], F32, name="res%d%d" % (q, h))
             for i in range(PACK):
-                nc.scalar.activation(out=res[q, h][:, i, :], in_=y_acc[q, h][:, i * TQ : (i + 1) * TQ], func=GELU, bias=bias[:, h, i : i + 1])
+                nc.scalar.activation(out=res[q, h][:, i, :], in_=y_acc[q, h, i], func=GELU, bias=bias[:, h, i : i + 1])
 
         def store_res(q, h):
             rows = out_0[h * PASS : (h + 1) * PASS, q * TQ : (q + 1) * TQ]
             nc.sync.dma_start(out=rows.rearrange("(p i) t -> p i t", i=PACK), in_=res[q, h][:])
 
-        def cast_res(q, h):
+        def cast_res(q, h, on_vector=1):
             res_bf[q, h] = stage.tile([P, PACK * TQ], BF16, name="res_bf%d%d" % (q, h), tag="res_bf", align_bytes=64)
-            nc.vector.tensor_copy(
-                out=res_bf[q, h][:].rearrange("p (m j i) -> p m i j", j=PACK, i=PACK),
-                in_=res[q, h][:].rearrange("p i (m j) -> p m i j", j=PACK),
-            )
+            dst = res_bf[q, h][:].rearrange("p (m j i) -> p m i j", j=PACK, i=PACK)
+            src = res[q, h][:].rearrange("p i (m j) -> p m i j", j=PACK)
+            if on_vector:
+                nc.vector.tensor_copy(out=dst, in_=src)
+            else:
+                nc.scalar.copy(out=dst, in_=src)
 
         def quantize_res(q, h):
-            if q not in res_codes:
-                res_codes[q] = keep.tile([P, 2, TQ], U32, name="res_codes%d" % q, align_bytes=64)
-            nc.vector.quantize_mx(out=res_codes[q][:, h, :].bitcast(E4M3), scales=res_scales[:, h, q * TQ : (q + 1) * TQ], in_=res_bf[q, h][:])
+            if (q // 2, h) not in res_codes:
+                res_codes[q // 2, h] = keep.tile([P, TH], U32, name="res_codes%d%d" % (q // 2, h), align_bytes=64)
+            tcols = slice((q % 2) * TQ, (q % 2 + 1) * TQ)
+            nc.vector.quantize_mx(out=res_codes[q // 2, h][:, tcols].bitcast(E4M3), scales=res_scales[:, h, q * TQ : (q + 1) * TQ], in_=res_bf[q, h][:])
 
-        def store_words(q):
-            words = out_1.rearrange("h p t i -> p h (t i)").bitcast(I32)
-            nc.sync.dma_start(out=words[:, :, q * TQ : (q + 1) * TQ], in_=res_codes[q][:].bitcast(I32))
+        def store_words(half, h):
+            words = out_1[h].rearrange("p t i -> p (t i)").bitcast(I32)
+            nc.sync.dma_start(out=words[:, half * TH : (half + 1) * TH], in_=res_codes[half, h][:].bitcast(I32))
 
-        steps = {"cs": cast_s, "cv": cast_v, "q": quantize, "dw": deal_words, "ds": deal_scales, "pc": project_c, "dc": drain_c, "px": project_x,
-                 "mu": multiply, "qh": quantize_h, "ph": project_h, "act": activate, "st": store_res, "cr": cast_res, "qr": quantize_res, "sw": store_words}
+        steps = {"cp": cast_pair, "cs": cast_s, "cv": cast_v, "q": quantize, "dw": deal_words, "ds": deal_scales, "pc": project_c, "dc": drain_c, "px": project_x,
+                 "mu": multiply, "qh": quantize_h, "ph": project_h, "p1": project_h_alone, "act": activate, "st": store_res, "cr": cast_res, "qr": quantize_res, "sw": store_words}
         for step in ORDER:
             steps[step[0]](*step[1:])
         for quad in range(4):

@@ -22,7 +22,7 @@ PASS = 512
 TQ = 128
 TH = 256
 
-SHARE = {'c': 16, 'wc0': 20, 'wc1': 20, 'wx00': 20, 'wx10': 20, 'wx01': 20, 'wx11': 20, 'wx02': 20, 'x00': 16, 'x01': 16, 'x02': 20, 'wx12': 20, 'x10': 0, 'x11': 0, 'x12': 20, 'r00': 32, 'r01': 32, 'r10': 32, 'r11': 32, 'r20': 32, 'r21': 32, 'r30': 32, 'r31': 32, 'y20': 0, 'y21': 0, 'y22': 0, 'y30': 0, 'y31': 0, 'y32': 0}
+SHARE = {'c': 16, 'wc0': 20, 'wc1': 20, 'wx00': 20, 'wx10': 20, 'wx01': 18, 'wx11': 18, 'wx02': 16, 'x00': 12, 'x01': 20, 'x02': 24, 'wx12': 20, 'x10': 0, 'x11': 0, 'x12': 20, 'r00': 32, 'r01': 32, 'r10': 32, 'r11': 32, 'r20': 32, 'r21': 32, 'r30': 32, 'r31': 32, 'y20': 0, 'y21': 0, 'y22': 0, 'y30': 0, 'y31': 0, 'y32': 0}
 LOADS = ['c', 'wc', 'wxg0', 'wxg1', 'wx02', 'x00', 'x01', 'x02', 'wx12', 'y20', 'y21', 'y22', 'y30', 'y31', 'y32']
 ORDER = [
     ('dw', 0, 0), ('dw', 0, 1), ('dw', 1, 0), ('dw', 1, 1), ('cs', 'c'), ('cv', 'c'),
@@ -30,26 +30,26 @@ ORDER = [
     ('q', 'wc1'), ('pc', 0), ('dc', 0, 0), ('dc', 0, 1), ('dc', 0, 2), ('cs', 'wx00'),
     ('cv', 'wx00'), ('cs', 'wx10'), ('cv', 'wx10'), ('q', 'wx00'), ('q', 'wx10'), ('ds',),
     ('dc', 0, 3), ('cs', 'wx01'), ('cv', 'wx01'), ('cs', 'wx11'), ('cv', 'wx11'), ('q', 'wx01'),
-    ('q', 'wx11'), ('cs', 'wx02'), ('cv', 'wx02'), ('q', 'wx02'), ('cs', 'x00'), ('cv', 'x00'),
+    ('q', 'wx11'), ('cs', 'wx02'), ('cv', 'wx02'), ('cv', 'x00'), ('q', 'wx02'), ('cs', 'x00'),
     ('q', 'x00'), ('px', 0, 0, 0, 1), ('cs', 'x01'), ('cv', 'x01'), ('q', 'x01'), ('pc', 1),
     ('cs', 'x02'), ('cv', 'x02'), ('q', 'x02'), ('px', 0, 0, 1, 12), ('px', 1, 0), ('dc', 1, 0),
-    ('dc', 1, 1), ('dc', 1, 2), ('cp', 'wx12', 0, 0), ('cp', 'wx12', 0, 1), ('cp', 'wx12', 1, 0), ('cp', 'wx12', 1, 1),
-    ('dc', 1, 3), ('q', 'wx12', 0, 4), ('q', 'wx12', 1, 4), ('q', 'wx12', 2, 4), ('q', 'wx12', 3, 4), ('px', 0, 1),
+    ('dc', 1, 1), ('dc', 1, 3, 1), ('dc', 1, 2), ('cp', 'wx12', 0, 0), ('cp', 'wx12', 0, 1), ('cp', 'wx12', 1, 0),
+    ('cp', 'wx12', 1, 1), ('q', 'wx12', 0, 4), ('q', 'wx12', 1, 4), ('q', 'wx12', 2, 4), ('q', 'wx12', 3, 4), ('px', 0, 1),
     ('px', 1, 1), ('cs', 'y20'), ('mu', 0, 0), ('mu', 0, 1), ('qh', 0, 0), ('cs', 'y21'),
     ('qh', 0, 1), ('ph', 0, 0), ('ph', 0, 1), ('mu', 1, 0), ('cs', 'y22'), ('q', 'y20'),
     ('q', 'y21'), ('q', 'y22'), ('px', 2, 0), ('px', 2, 1), ('mu', 1, 1), ('qh', 1, 0),
     ('cs', 'y30'), ('qh', 1, 1), ('act', 0, 0), ('st', 0, 0), ('cs', 'y31'), ('act', 0, 1),
     ('st', 0, 1), ('cs', 'y32'), ('cr', 0, 0), ('q', 'y30'), ('q', 'y31'), ('qr', 0, 0),
-    ('mu', 2, 0), ('cr', 0, 1), ('mu', 2, 1), ('qr', 0, 1), ('q', 'y32'), ('ph', 1, 0),
-    ('ph', 1, 1), ('px', 3, 0), ('qh', 2, 0), ('qh', 2, 1), ('act', 1, 0), ('st', 1, 0),
-    ('act', 1, 1), ('st', 1, 1), ('ph', 2, 0), ('px', 3, 1), ('ph', 2, 1), ('cr', 1, 0),
-    ('cr', 1, 1), ('mu', 3, 0), ('qr', 1, 0), ('qr', 1, 1), ('sw', 0, 0), ('sw', 0, 1),
-    ('qh', 3, 0), ('act', 2, 0), ('st', 2, 0), ('mu', 3, 1), ('cr', 2, 0), ('qh', 3, 1),
+    ('mu', 2, 0), ('mu', 2, 1), ('q', 'y32'), ('ph', 1, 0), ('ph', 1, 1), ('px', 3, 0),
+    ('qh', 2, 0), ('qh', 2, 1), ('cr', 0, 1), ('act', 1, 0), ('st', 1, 0), ('act', 1, 1),
+    ('cr', 1, 1, 0), ('st', 1, 1), ('ph', 2, 0), ('px', 3, 1), ('ph', 2, 1), ('cr', 1, 0),
+    ('qr', 0, 1), ('mu', 3, 0), ('qr', 1, 0), ('qr', 1, 1), ('sw', 0, 0), ('sw', 0, 1),
+    ('qh', 3, 0), ('act', 2, 0), ('st', 2, 0), ('mu', 3, 1), ('qh', 3, 1), ('cr', 2, 0, 0),
     ('p1', 3, 0, 0, 0), ('p1', 3, 0, 1, 0), ('p1', 3, 0, 2, 0), ('p1', 3, 0, 3, 0), ('p1', 3, 1, 0, 0), ('p1', 3, 1, 1, 0),
     ('p1', 3, 0, 0, 1), ('p1', 3, 0, 1, 1), ('p1', 3, 0, 2, 1), ('p1', 3, 0, 3, 1), ('p1', 3, 1, 0, 1), ('p1', 3, 1, 1, 1),
     ('act', 2, 1), ('st', 2, 1), ('p1', 3, 1, 2, 0), ('p1', 3, 1, 2, 1), ('p1', 3, 1, 3, 0), ('p1', 3, 1, 3, 1),
     ('qr', 2, 0), ('cr', 2, 1), ('qr', 2, 1), ('act', 3, 0), ('st', 3, 0), ('act', 3, 1),
-    ('st', 3, 1), ('cr', 3, 0), ('qr', 3, 0), ('sw', 1, 0), ('cr', 3, 1), ('qr', 3, 1),
+    ('st', 3, 1), ('cr', 3, 0), ('cr', 3, 1), ('qr', 3, 0), ('sw', 1, 0), ('qr', 3, 1),
     ('sw', 1, 1),
 ]
 
@@ -190,8 +190,11 @@ def tile_mix_bilin_fm_pl_gelu_kernel(tc, x, wx, c, wc, w_words, w_scales, b, out
 
         pc_acc = {}
 
-        def drain_c(a, j):
-            nc.scalar.copy(out=pc[a][:, j, :], in_=pc_acc[a, j][:])
+        def drain_c(a, j, on_vector=0):
+            if on_vector:
+                nc.vector.tensor_copy(out=pc[a][:, j, :], in_=pc_acc[a, j][:])
+            else:
+                nc.scalar.copy(out=pc[a][:, j, :], in_=pc_acc[a, j][:])
 
         px_acc, h_bf, h_codes, h_scales = {}, {}, {}, {}
 

from contextlib import ExitStack

import concourse.mybir as mybir

K, L, R, M, T = 1536, 512, 1024, 1024, 512
FLOPS = 2 * T * (K * R + L * R + R * M)

F32 = mybir.dt.float32
BF16 = mybir.dt.bfloat16
U32 = mybir.dt.uint32
I32 = mybir.dt.int32
U8 = mybir.dt.uint8
E4M3 = mybir.dt.float8_e4m3fn_x4
E5M2 = mybir.dt.float8_e5m2_x4
E2M1 = mybir.dt.float4_e2m1fn_x4
GELU = mybir.ActivationFunctionType.Gelu_apprx_tanh
MULT = mybir.AluOpType.mult

P = 128
PACK = 4
PASS = 512
TQ = 128
TH = 256

SHARE = {'c': 16, 'wc0': 20, 'wc1': 20, 'wx00': 20, 'wx10': 20, 'wx01': 18, 'wx11': 18, 'wx02': 16, 'x00': 12, 'x01': 20, 'x02': 24, 'wx12': 20, 'x10': 0, 'x11': 0, 'x12': 20, 'r00': 32, 'r01': 32, 'r10': 32, 'r11': 32, 'r20': 32, 'r21': 32, 'r30': 32, 'r31': 32, 'y20': 0, 'y21': 0, 'y22': 0, 'y30': 0, 'y31': 0, 'y32': 0}
LOADS = ['c', 'wc', 'wxg0', 'wxg1', 'wx02', 'x00', 'x01', 'x02', 'wx12', 'y20', 'y21', 'y22', 'y30', 'y31', 'y32']
ORDER = [
    ('dw', 0, 0), ('dw', 0, 1), ('dw', 1, 0), ('dw', 1, 1), ('cs', 'c'), ('cv', 'c'),
    ('q', 'c'), ('cs', 'wc0'), ('cv', 'wc0'), ('cs', 'wc1'), ('cv', 'wc1'), ('q', 'wc0'),
    ('q', 'wc1'), ('pc', 0), ('dc', 0, 0), ('dc', 0, 1), ('dc', 0, 2), ('cs', 'wx00'),
    ('cv', 'wx00'), ('cs', 'wx10'), ('cv', 'wx10'), ('q', 'wx00'), ('q', 'wx10'), ('ds',),
    ('dc', 0, 3), ('cs', 'wx01'), ('cv', 'wx01'), ('cs', 'wx11'), ('cv', 'wx11'), ('q', 'wx01'),
    ('q', 'wx11'), ('cs', 'wx02'), ('cv', 'wx02'), ('cv', 'x00'), ('q', 'wx02'), ('cs', 'x00'),
    ('q', 'x00'), ('px', 0, 0, 0, 1), ('cs', 'x01'), ('cv', 'x01'), ('q', 'x01'), ('pc', 1),
    ('cs', 'x02'), ('cv', 'x02'), ('q', 'x02'), ('px', 0, 0, 1, 12), ('px', 1, 0), ('dc', 1, 0),
    ('dc', 1, 1), ('dc', 1, 3, 1), ('dc', 1, 2), ('cp', 'wx12', 0, 0), ('cp', 'wx12', 0, 1), ('cp', 'wx12', 1, 0),
    ('cp', 'wx12', 1, 1), ('q', 'wx12', 0, 4), ('q', 'wx12', 1, 4), ('q', 'wx12', 2, 4), ('q', 'wx12', 3, 4), ('px', 0, 1),
    ('px', 1, 1), ('cs', 'y20'), ('mu', 0, 0), ('mu', 0, 1), ('qh', 0, 0), ('cs', 'y21'),
    ('qh', 0, 1), ('ph', 0, 0), ('ph', 0, 1), ('mu', 1, 0), ('cs', 'y22'), ('q', 'y20'),
    ('q', 'y21'), ('q', 'y22'), ('px', 2, 0), ('px', 2, 1), ('mu', 1, 1), ('qh', 1, 0),
    ('cs', 'y30'), ('qh', 1, 1), ('act', 0, 0), ('st', 0, 0), ('cs', 'y31'), ('act', 0, 1),
    ('st', 0, 1), ('cs', 'y32'), ('cr', 0, 0), ('q', 'y30'), ('q', 'y31'), ('qr', 0, 0),
    ('mu', 2, 0), ('mu', 2, 1), ('q', 'y32'), ('ph', 1, 0), ('ph', 1, 1), ('px', 3, 0),
    ('qh', 2, 0), ('qh', 2, 1), ('cr', 0, 1), ('act', 1, 0), ('st', 1, 0), ('act', 1, 1),
    ('cr', 1, 1, 0), ('st', 1, 1), ('ph', 2, 0), ('px', 3, 1), ('ph', 2, 1), ('cr', 1, 0),
    ('qr', 0, 1), ('mu', 3, 0), ('qr', 1, 0), ('qr', 1, 1), ('sw', 0, 0), ('sw', 0, 1),
    ('qh', 3, 0), ('act', 2, 0), ('st', 2, 0), ('mu', 3, 1), ('qh', 3, 1), ('cr', 2, 0, 0),
    ('p1', 3, 0, 0, 0), ('p1', 3, 0, 1, 0), ('p1', 3, 0, 2, 0), ('p1', 3, 0, 3, 0), ('p1', 3, 1, 0, 0), ('p1', 3, 1, 1, 0),
    ('p1', 3, 0, 0, 1), ('p1', 3, 0, 1, 1), ('p1', 3, 0, 2, 1), ('p1', 3, 0, 3, 1), ('p1', 3, 1, 0, 1), ('p1', 3, 1, 1, 1),
    ('act', 2, 1), ('st', 2, 1), ('p1', 3, 1, 2, 0), ('p1', 3, 1, 2, 1), ('p1', 3, 1, 3, 0), ('p1', 3, 1, 3, 1),
    ('qr', 2, 0), ('cr', 2, 1), ('qr', 2, 1), ('act', 3, 0), ('st', 3, 0), ('act', 3, 1),
    ('st', 3, 1), ('cr', 3, 0), ('cr', 3, 1), ('qr', 3, 0), ('sw', 1, 0), ('qr', 3, 1),
    ('sw', 1, 1),
]


def tile_mix_bilin_fm_pl_gelu_kernel(tc, x, wx, c, wc, w_words, w_scales, b, out_0, out_1, out_2):
    nc = tc.nc
    with ExitStack() as ctx:
        keep = ctx.enter_context(tc.tile_pool(name="keep", bufs=1))
        stage = ctx.enter_context(tc.tile_pool(name="stage", bufs=4))
        psum = ctx.enter_context(tc.psum_pool(name="psum", bufs=1))
        ctx.enter_context(tc.manual_schedule())

        banks_taken = []

        def take_bank(name):
            tag = "bank%d" % (len(banks_taken) % 8)
            banks_taken.append(name)
            return psum.tile([P, PASS], F32, name=name, tag=tag)

        raw, grouped, codes, scales = {}, {}, {}, {}

        def load(key, rows):
            width = rows.shape[1]
            raw[key] = keep.tile([P, PACK, width], F32, name="raw_" + key)
            nc.sync.dma_start(out=raw[key][:], in_=rows.rearrange("(p k) n -> p k n", k=PACK))

        def cast_views(key):
            width = raw[key].shape[2]
            if key not in grouped:
                grouped[key] = stage.tile([P, PACK * width], BF16, name="grouped_" + key, tag="grouped%d" % width, align_bytes=64)
            if key.startswith("w"):
                dst = grouped[key][:].rearrange("p (j m k) -> p m k j", j=PACK, k=PACK)
            else:
                dst = grouped[key][:].rearrange("p (m j k) -> p m k j", j=PACK, k=PACK)
            src = raw[key][:, :, :].rearrange("p k (m j) -> p m k j", j=PACK)
            groups = width // PACK
            return dst, src, groups * SHARE[key] // 32, groups

        def cast_s(key):
            dst, src, cut, groups = cast_views(key)
            if cut < groups:
                nc.scalar.copy(out=dst[:, cut:groups], in_=src[:, cut:groups])

        def cast_v(key):
            dst, src, cut, groups = cast_views(key)
            if cut > 0:
                nc.vector.tensor_copy(out=dst[:, 0:cut], in_=src[:, 0:cut])

        def cast_pair(key, pair, on_vector):
            if key not in grouped:
                grouped[key] = stage.tile([P, PACK * PASS], BF16, name="grouped_" + key, tag="grouped%d" % PASS, align_bytes=64)
            dst = grouped[key][:].rearrange("p (u l m k) -> p u m k l", u=2, l=2, k=PACK)[:, pair]
            src = raw[key][:, :, :].rearrange("p k (m u l) -> p u m k l", u=2, l=2)[:, pair]
            cut = P * SHARE[key] // 32
            if on_vector:
                nc.vector.tensor_copy(out=dst[:, 0:cut], in_=src[:, 0:cut])
            else:
                nc.scalar.copy(out=dst[:, cut:P], in_=src[:, cut:P])

        def quantize(key, part=0, parts=1):
            width = raw[key].shape[2]
            fmt = E5M2 if key == "c" else E4M3
            if key not in codes:
                codes[key] = keep.tile([P, width], U32, name="codes_" + key, align_bytes=64)
                scales[key] = keep.tile([P, width], U8, name="scales_" + key, align_bytes=64)
            lo, hi = part * width // parts, (part + 1) * width // parts
            nc.vector.quantize_mx(out=codes[key][:, lo:hi].bitcast(fmt), scales=scales[key][:, lo:hi], in_=grouped[key][:, PACK * lo : PACK * hi])

        ws_raw = keep.tile([P, 2, M], U8, name="ws_raw")
        nc.vector.memset(ws_raw[:].rearrange("p a n -> p (a n)").bitcast(I32), 0)
        warm = keep.tile([P, 8], F32, name="warm")
        warm_out = keep.tile([P, 8], F32, name="warm_out")
        nc.vector.memset(warm[:], 0.0)
        bias = keep.tile([P, 2, PACK], F32, name="bias")
        nc.scalar.dma_start(out=bias[:], in_=b.rearrange("(h p i) -> p h i", h=2, i=PACK))
        for quad in range(4):
            nc.gpsimd.dma_start(
                out=ws_raw[32 * quad : 32 * quad + 4, :, :].bitcast(I32),
                in_=w_scales[:, 4 * quad : 4 * quad + 4, :].rearrange("a r n -> r a n").bitcast(I32),
            )
        nc.scalar.activation(out=warm_out[:, 0:1], in_=warm[:, 0:1], func=GELU)
        ww_raw = keep.tile([P, 2, 2 * M], U8, name="ww_raw")
        nc.sync.dma_start(out=ww_raw[:].bitcast(I32), in_=w_words.rearrange("a p n -> p a n").bitcast(I32))

        def load_wx(a, g):
            load("wx%d%d" % (a, g), wx[g * PASS : (g + 1) * PASS, a * PASS : (a + 1) * PASS])

        def load_x(half, g):
            load("x%d%d" % (half, g), x[g * PASS : (g + 1) * PASS, half * TH : (half + 1) * TH])

        for key in LOADS:
            if key == "c":
                load("c", c)
            elif key == "wc":
                load(key, wc)
                raw["wc0"], raw["wc1"] = raw[key][:, :, 0:PASS], raw[key][:, :, PASS : 2 * PASS]
            elif key.startswith("wxg"):
                g = int(key[3])
                load(key, wx[g * PASS : (g + 1) * PASS, :])
                raw["wx0%d" % g], raw["wx1%d" % g] = raw[key][:, :, 0:PASS], raw[key][:, :, PASS : 2 * PASS]
            elif key.startswith("wc"):
                load(key, wc[:, int(key[2]) * PASS : (int(key[2]) + 1) * PASS])
            elif key.startswith("wx"):
                load_wx(int(key[2]), int(key[3]))
            elif key.startswith("y"):
                q, g = int(key[1]), int(key[2])
                load(key, x[g * PASS : (g + 1) * PASS, q * TQ : (q + 1) * TQ])
            else:
                load_x(int(key[1]), int(key[2]))

        ww = keep.tile([P, 2, 2 * M], U8, name="ww", align_bytes=64)
        ws = keep.tile([P, 2, M], U8, name="ws", align_bytes=64)

        def deal_words(a, h):
            cols = slice(2 * PASS * h, 2 * PASS * (h + 1))
            nc.vector.tensor_copy(
                out=ww[:, a, cols].rearrange("p (i m e) -> p i m e", i=PACK, e=2),
                in_=ww_raw[:, a, cols].rearrange("p (m i e) -> p i m e", i=PACK, e=2),
            )

        def deal_scales():
            nc.vector.tensor_copy(
                out=ws[:].rearrange("p a (h i m) -> p (a h) i m", h=2, i=PACK),
                in_=ws_raw[:].rearrange("p a (h m i) -> p (a h) i m", h=2, i=PACK),
            )

        pc = {}

        def project_c(a):
            pc[a] = keep.tile([P, PACK, T], F32, name="pc%d" % a)
            for j in range(PACK):
                acc = take_bank("pc_acc%d%d" % (a, j))
                cols = slice(j * P, (j + 1) * P)
                key = "wc%d" % a
                nc.tensor.matmul_mx(out=acc[:], lhsT=codes[key][:, cols].bitcast(E4M3), lhsT_scale=scales[key][:, cols],
                                    rhs=codes["c"][:].bitcast(E5M2), rhs_scale=scales["c"][:], start=True, stop=True)
                pc_acc[a, j] = acc

        pc_acc = {}

        def drain_c(a, j, on_vector=0):
            if on_vector:
                nc.vector.tensor_copy(out=pc[a][:, j, :], in_=pc_acc[a, j][:])
            else:
                nc.scalar.copy(out=pc[a][:, j, :], in_=pc_acc[a, j][:])

        px_acc, h_bf, h_codes, h_scales = {}, {}, {}, {}

        def project_x(q, a, first=0, last=12):
            if first == 0:
                px_acc[q, a] = take_bank("px_acc%d%d" % (q, a))
            acc = px_acc[q, a]
            alone = "y%d0" % q in LOADS
            tcols = slice(0, TQ) if alone else slice((q % 2) * TQ, (q % 2 + 1) * TQ)
            for n in range(first, last):
                j, g = divmod(n, 3)
                cols = slice(j * P, (j + 1) * P)
                wkey, xkey = "wx%d%d" % (a, g), ("y%d%d" % (q, g) if alone else "x%d%d" % (q // 2, g))
                nc.tensor.matmul_mx(out=acc[:, cols], lhsT=codes[wkey][:, cols].bitcast(E4M3), lhsT_scale=scales[wkey][:, cols],
                                    rhs=codes[xkey][:, tcols].bitcast(E4M3), rhs_scale=scales[xkey][:, tcols],
                                    start=(g == 0), stop=(g == 2))

        def multiply(q, a):
            h_bf[q, a] = stage.tile([P, PACK * TQ], BF16, name="h_bf%d%d" % (q, a), tag="h_bf", align_bytes=64)
            nc.vector.tensor_tensor(
                out=h_bf[q, a][:].rearrange("p (m i j) -> p m j i", i=PACK, j=PACK),
                in0=px_acc[q, a][:].rearrange("p (j m i) -> p m j i", j=PACK, i=PACK),
                in1=pc[a][:, :, q * TQ : (q + 1) * TQ].rearrange("p j (m i) -> p m j i", i=PACK),
                op=MULT,
            )

        def quantize_h(q, a):
            h_codes[q, a] = keep.tile([P, TQ], U32, name="h_codes%d%d" % (q, a), align_bytes=64)
            h_scales[q, a] = keep.tile([P, TQ], U8, name="h_scales%d%d" % (q, a), align_bytes=64)
            nc.vector.quantize_mx(out=h_codes[q, a][:].bitcast(E4M3), scales=h_scales[q, a][:], in_=h_bf[q, a][:])

        y_acc, res, res_bf, res_codes = {}, {}, {}, {}
        res_scales = keep.tile([P, 2, T], U8, name="res_scales", align_bytes=64)

        def out_pass(q, h, i, a):
            n0 = h * PASS + i * P
            nc.tensor.matmul_mx(out=y_acc[q, h, i], lhsT=ww[:, a, 2 * n0 : 2 * (n0 + P)].bitcast(E2M1),
                                lhsT_scale=ws[:, a, n0 : n0 + P], rhs=h_codes[q, a][:].bitcast(E4M3),
                                rhs_scale=h_scales[q, a][:], start=(a == 0), stop=(a == 1))

        def project_h(q, h):
            acc = take_bank("y_acc%d%d" % (q, h))
            for i in range(PACK):
                y_acc[q, h, i] = acc[:, i * TQ : (i + 1) * TQ]
                for a in range(2):
                    out_pass(q, h, i, a)

        def project_h_alone(q, h, i, a):
            if a == 0:
                acc = take_bank("y_acc%d%d%d" % (q, h, i))
                y_acc[q, h, i] = acc[:, 0:TQ]
            out_pass(q, h, i, a)

        def activate(q, h):
            res[q, h] = keep.tile([P, PACK, TQ], F32, name="res%d%d" % (q, h))
            for i in range(PACK):
                nc.scalar.activation(out=res[q, h][:, i, :], in_=y_acc[q, h, i], func=GELU, bias=bias[:, h, i : i + 1])

        def store_res(q, h):
            rows = out_0[h * PASS : (h + 1) * PASS, q * TQ : (q + 1) * TQ]
            nc.sync.dma_start(out=rows.rearrange("(p i) t -> p i t", i=PACK), in_=res[q, h][:])

        def cast_res(q, h, on_vector=1):
            res_bf[q, h] = stage.tile([P, PACK * TQ], BF16, name="res_bf%d%d" % (q, h), tag="res_bf", align_bytes=64)
            dst = res_bf[q, h][:].rearrange("p (m j i) -> p m i j", j=PACK, i=PACK)
            src = res[q, h][:].rearrange("p i (m j) -> p m i j", j=PACK)
            if on_vector:
                nc.vector.tensor_copy(out=dst, in_=src)
            else:
                nc.scalar.copy(out=dst, in_=src)

        def quantize_res(q, h):
            if (q // 2, h) not in res_codes:
                res_codes[q // 2, h] = keep.tile([P, TH], U32, name="res_codes%d%d" % (q // 2, h), align_bytes=64)
            tcols = slice((q % 2) * TQ, (q % 2 + 1) * TQ)
            nc.vector.quantize_mx(out=res_codes[q // 2, h][:, tcols].bitcast(E4M3), scales=res_scales[:, h, q * TQ : (q + 1) * TQ], in_=res_bf[q, h][:])

        def store_words(half, h):
            words = out_1[h].rearrange("p t i -> p (t i)").bitcast(I32)
            nc.sync.dma_start(out=words[:, half * TH : (half + 1) * TH], in_=res_codes[half, h][:].bitcast(I32))

        steps = {"cp": cast_pair, "cs": cast_s, "cv": cast_v, "q": quantize, "dw": deal_words, "ds": deal_scales, "pc": project_c, "dc": drain_c, "px": project_x,
                 "mu": multiply, "qh": quantize_h, "ph": project_h, "p1": project_h_alone, "act": activate, "st": store_res, "cr": cast_res, "qr": quantize_res, "sw": store_words}
        for step in ORDER:
            steps[step[0]](*step[1:])
        for quad in range(4):
            nc.sync.dma_start(
                out=out_2[:, 4 * quad : 4 * quad + 4, :].rearrange("h r t -> r h t").bitcast(I32),
                in_=res_scales[32 * quad : 32 * quad + 4, :, :].bitcast(I32),
            )
